import numpy as np
import ml_dtypes


def mxq(x, axis, fmt="e4m3"):
    dtype, down = {"e4m3": (ml_dtypes.float8_e4m3fn, 7), "e5m2": (ml_dtypes.float8_e5m2, 14)}[fmt]
    v = np.moveaxis(np.asarray(x, np.float32).astype(ml_dtypes.bfloat16).astype(np.float64), axis, -1)
    blocks = v.reshape(v.shape[:-1] + (-1, 32))
    amax = np.abs(blocks).max(-1, keepdims=True)
    byte = np.maximum(np.where(amax > 0, np.frexp(amax)[1] - 1 + 127, 0) - down, 1)
    scale = np.exp2(byte - 127.0)
    codes = (blocks / scale).astype(np.float32).astype(dtype).astype(np.float64)
    return np.moveaxis((codes * scale).reshape(v.shape), -1, axis)


WIDE = False


def mx_kscale(k):
    if not WIDE:
        return np.ones(k)
    levels = np.array([10, -10, 5, -5, 0])
    if k % 512:
        return np.exp2(np.random.permutation(np.resize(levels, k // 32))).repeat(32)
    a = np.empty((k // 512, 16))
    for p in range(k // 512):
        a[p, :8] = np.random.permutation(np.resize(levels, 8))
        for g in range(8):
            far = levels[np.abs(levels - a[p, g]) >= 10]
            a[p, g + 8] = far[np.random.randint(len(far))]
    return np.exp2(a.ravel()).repeat(32)


def f64(x):
    return np.asarray(x).astype(np.float64)


def striped8(idx):
    return np.concatenate([x.reshape(-1, 16).T for x in idx]).astype(np.uint16)


def runs(offs, k):
    lists = np.stack([offs[16 * r : 16 * r + 16].T.reshape(-1) for r in range(8)]).astype(np.int64)
    return lists[np.arange(k) % 512 // 64]


def pack_weight(w):
    k, n = w.shape
    w = f64(np.asarray(w, np.float32).astype(ml_dtypes.bfloat16)).reshape(k // 32, 32, n)
    amax = np.abs(w).max(1)
    byte = np.clip(np.where(amax > 0, np.frexp(amax)[1] - 1 + 127 - 7, 1), 1, 254)
    scaled = (w * np.exp2(127.0 - byte)[:, None, :]).reshape(k, n).astype(np.float32)
    words = np.ascontiguousarray(scaled.reshape(k // 512, 128, 4, n).transpose(0, 1, 3, 2)).astype(ml_dtypes.float8_e4m3fn).view(np.uint8)
    return words, np.ascontiguousarray(byte.astype(np.uint8).reshape(k // 512, 16, n))


def unpack_weight(words, scales):
    g, p, n, _ = words.shape
    vals = np.ascontiguousarray(words).view(ml_dtypes.float8_e4m3fn).astype(np.float64) * np.repeat(np.exp2(scales.astype(np.float64) - 127.0), 8, axis=1)[..., None]
    return vals.transpose(0, 1, 3, 2).reshape(g * 512, n)


def relu(v):
    return np.maximum(v, 0.0)

def planes(y):
    n, m = y.shape
    v = y.astype(np.float32).astype(ml_dtypes.bfloat16).astype(np.float64).reshape(n // 32, 32, m)
    top = np.abs(v).max(1)
    byte = np.clip(np.where(top > 0, np.frexp(top)[1] - 1 + 127 - 7, 1), 1, 254)
    codes = (v * np.exp2(127.0 - byte)[:, None, :]).reshape(n, m).astype(np.float32).astype(ml_dtypes.float8_e4m3fn).view(np.uint8)
    words = codes.reshape(n // 512, 128, 4, m).transpose(0, 1, 3, 2)
    return np.ascontiguousarray(words), np.ascontiguousarray(byte.astype(np.uint8).reshape(n // 512, 16, m))


K, T, S, N, H = 512, 2048, 512, 512, 512


def setup_inputs():
    n = np.random.standard_normal
    s = mx_kscale(K)[:, None]
    u = mx_kscale(H)
    packed_xT = pack_weight(n((K, T)) * s)
    packed_w1 = pack_weight(n((K, H)) / np.sqrt(K) / s)
    packed_w2 = pack_weight(n((H, N)) / np.sqrt(H) / u[:, None])
    return {
        "x_words": packed_xT[0],
        "x_scales": packed_xT[1],
        "w1_words": packed_w1[0],
        "w1_scales": packed_w1[1],
        "gn": (np.random.uniform(0.5, 1.5, (H, 1)) * u[:, None]).astype(np.float32),
        "w2_words": packed_w2[0],
        "w2_scales": packed_w2[1],
        "offs": striped8(np.random.randint(0, T, (8, S))),
        "n1": striped8(np.stack([np.random.permutation(S) for _ in range(8)])),
        "n2": striped8(np.stack([np.random.permutation(S) for _ in range(8)])),
        "n3": striped8(np.stack([np.random.permutation(S) for _ in range(8)])),
        "n4": striped8(np.stack([np.random.permutation(S) for _ in range(8)])),
    }


def reference(x_words, x_scales, w1_words, w1_scales, gn, w2_words, w2_scales, offs, n1, n2, n3, n4):
    xq = unpack_weight(x_words, x_scales)[np.arange(K)[:, None], runs(offs, K)]
    y = unpack_weight(w1_words, w1_scales).T @ xq
    pa = y - (y[np.arange(H)[:, None], runs(n1, H)])
    pb = y[np.arange(H)[:, None], runs(n2, H)] - y
    z = f64(gn) * (relu(np.minimum(pa, pb)) - (relu(-1.0 * np.maximum(pa, pb))))
    h = unpack_weight(w2_words, w2_scales).T @ mxq(z, 0, "e4m3")
    st = h - (h[np.arange(N)[:, None], runs(n3, N)])
    out_0 = np.maximum(st, st[np.arange(N)[:, None], runs(n4, N)])
    return (out_0,) + planes(out_0)

@@ -1,0 +1,254 @@
+from contextlib import ExitStack
+
+import concourse.mybir as mybir
+
+K, T, S, H, N = 512, 2048, 512, 512, 512
+FLOPS = 2 * K * H * S + 2 * H * N * S
+
+F32 = mybir.dt.float32
+BF16 = mybir.dt.bfloat16
+I32 = mybir.dt.int32
+U32 = mybir.dt.uint32
+U16 = mybir.dt.uint16
+U8 = mybir.dt.uint8
+FP8X4 = mybir.dt.float8_e4m3fn_x4
+ALU = mybir.AluOpType
+COPY = mybir.ActivationFunctionType.Copy
+
+P = 128
+PACK = 4
+HALF = S // 2
+LIST_ROWS = 16
+HALVES = [(0, HALF), (HALF, HALF)]
+PIECES = [(0, 256), (256, 128), (384, 128)]
+
+
+def tile_picked_hashminmodhopmx_none_po_kernel(
+    tc, x_words, x_scales, w1_words, w1_scales, gn, w2_words, w2_scales, offs, n1, n2, n3, n4, out_0, out_1, out_2
+):
+    nc = tc.nc
+
+    with ExitStack() as ctx:
+        keep = ctx.enter_context(tc.tile_pool(name="keep", bufs=1))
+        psum = ctx.enter_context(tc.psum_pool(name="psum", bufs=1))
+
+        def sb(name, shape, dtype):
+            return keep.tile(shape, dtype, name=name, align_bytes=64)
+
+        def bank(number, name):
+            return psum.tile([P, 512], F32, name=name, tag="bank%d" % number)
+
+        def words_view(dram):
+            return dram[0].rearrange("p n t -> p (n t)").bitcast(I32)
+
+        def entries(lists, start, count):
+            return lists[:, start // LIST_ROWS : (start + count) // LIST_ROWS]
+
+        lists = {name: sb("list_" + name, [P, S // LIST_ROWS], U16) for name in ("offs", "n1", "n2", "n3", "n4")}
+        x_table = sb("x_table", [P, T], U32)
+        x_scale_table = sb("x_scale_table", [P, T], U8)
+        w_raw = [sb("w_raw%d" % i, [P, 512], U32) for i in range(2)]
+        w_scale_raw = sb("w_scale_raw", [P, 512], U8)
+        w_codes = [sb("w_codes%d" % i, [P, 512], U32) for i in range(2)]
+        w_scale = [sb("w_scale%d" % i, [P, 512], U8) for i in range(2)]
+        x_codes = sb("x_codes", [P, S], U32)
+        x_scale_picked = sb("x_scale_picked", [P, S], U8)
+        x_scale = sb("x_scale", [P, S], U8)
+        gain = sb("gain", [P, PACK], F32)
+        minus_gain = sb("minus_gain", [P, PACK], F32)
+        warm = sb("warm", [P, 8], F32)
+        warm_out = sb("warm_out", [P, 8], F32)
+
+        nc.vector.memset(warm[:], 0.0)
+        nc.vector.memset(x_scale[:].bitcast(I32), 0)
+
+        def load_weight_scales(queue, dram, q):
+            rows = dram[0, 4 * q : 4 * q + 4, :].bitcast(I32)
+            queue.dma_start(w_scale_raw[32 * q : 32 * q + 32, :].bitcast(I32), rows.unsqueeze(0).broadcast_to([8, 4, 128]))
+
+        nc.sync.dma_start(
+            x_scale_table[:].bitcast(I32), x_scales[0].bitcast(I32).unsqueeze(1).broadcast_to([16, 8, T // 4])
+        )
+        nc.sync.dma_start(lists["offs"][:], offs)
+        for q in range(4):
+            load_weight_scales(nc.sync if q < 2 else nc.gpsimd, w1_scales, q)
+        nc.sync.dma_start(lists["n1"][:], n1)
+        nc.sync.dma_start(lists["n2"][:], n2)
+        nc.sync.dma_start(w_raw[0][:].bitcast(I32), words_view(w1_words))
+        nc.sync.dma_start(x_table[:].bitcast(I32), words_view(x_words))
+        nc.sync.dma_start(lists["n3"][:], n3)
+        nc.sync.dma_start(lists["n4"][:], n4)
+        nc.sync.dma_start(w_raw[1][:].bitcast(I32), words_view(w2_words))
+        nc.scalar.activation(warm_out[:], warm[:], COPY)
+        nc.gpsimd.dma_start(gain[:], gn.rearrange("(p t) o -> p (t o)", t=PACK))
+        nc.gpsimd.tensor_scalar(minus_gain[:], gain[:], -1.0, 0.0, ALU.mult, ALU.add)
+
+        def deal_words(i):
+            nc.vector.tensor_copy(
+                w_codes[i][:].bitcast(I32).rearrange("p (t m) -> p t m", t=PACK),
+                w_raw[i][:].bitcast(I32).rearrange("p (m t) -> p t m", t=PACK),
+            )
+
+        def deal_scales(i):
+            nc.vector.tensor_copy(
+                w_scale[i][:].rearrange("p (t m) -> p t m", t=PACK),
+                w_scale_raw[:].rearrange("p (m t) -> p t m", t=PACK),
+            )
+
+        nc.vector.tensor_copy(x_scale_picked[:], x_scale_table[:].indirect(lists["offs"][:]))
+        for j in range(4):
+            nc.scalar.dma_start(x_scale[j:P:32, :].bitcast(I32), x_scale_picked[8 * j : P : 32, :].bitcast(I32))
+        deal_words(0)
+        deal_scales(0)
+        nc.vector.tensor_copy(x_codes[:], x_table[:].indirect(lists["offs"][:]))
+        for q in range(4):
+            load_weight_scales(nc.sync, w2_scales, q)
+        deal_words(1)
+        deal_scales(1)
+
+        def product(out, i, t, codes, scales):
+            cols = slice(t * P, (t + 1) * P)
+            nc.tensor.matmul_mx(
+                out=out,
+                lhsT=w_codes[i][:, cols].bitcast(FP8X4),
+                lhsT_scale=w_scale[i][:, cols],
+                rhs=codes.bitcast(FP8X4),
+                rhs_scale=scales,
+                start=True,
+                stop=True,
+            )
+
+        y = [sb("y%d" % t, [P, S], F32) for t in range(PACK)]
+        minus_y = [sb("minus_y%d" % t, [P, S], F32) for t in range(PACK)]
+        first = [bank(h, "y0_%d" % h) for h in range(2)]
+        for h, (c0, n) in enumerate(HALVES):
+            product(first[h][:, 0:n], 0, 0, x_codes[:, c0 : c0 + n], x_scale[:, c0 : c0 + n])
+        nc.scalar.activation(minus_y[0][:, 0:HALF], first[0][:, 0:HALF], COPY, scale=minus_gain[:, 0:1])
+        nc.vector.tensor_scalar(minus_y[0][:, HALF:S], first[1][:, 0:HALF], minus_gain[:, 0:1], None, ALU.mult)
+        nc.scalar.activation(y[0][:, 0:HALF], first[0][:, 0:HALF], COPY, scale=gain[:, 0:1])
+        nc.scalar.activation(y[0][:, HALF:S], first[1][:, 0:HALF], COPY, scale=gain[:, 0:1])
+        for t in range(1, PACK):
+            acc = bank(1 + t, "y_acc%d" % t)
+            product(acc[:], 0, t, x_codes[:], x_scale[:])
+            nc.scalar.activation(minus_y[t][:], acc[:], COPY, scale=minus_gain[:, t : t + 1])
+            nc.scalar.activation(y[t][:], acc[:], COPY, scale=gain[:, t : t + 1])
+
+        pa = [sb("pa%d" % h, [P, PACK, HALF], F32) for h in range(2)]
+        pb = [sb("pb%d" % h, [P, PACK, HALF], F32) for h in range(2)]
+        low = [sb("low%d" % c, [P, PACK, n], F32) for c, (c0, n) in enumerate(PIECES)]
+        z = [sb("z%d" % c, [P, PACK, n], BF16) for c, (c0, n) in enumerate(PIECES)]
+        z_woven = [sb("z_woven%d" % c, [P, n, PACK], BF16) for c, (c0, n) in enumerate(PIECES)]
+        z_codes = [sb("z_codes%d" % c, [P, n], U32) for c, (c0, n) in enumerate(PIECES)]
+        z_scale = [sb("z_scale%d" % c, [P, n], U8) for c, (c0, n) in enumerate(PIECES)]
+        h_plain = [sb("h%d" % t, [P, S], F32) for t in range(PACK)]
+        minus_h = [sb("minus_h%d" % t, [P, S], F32) for t in range(PACK)]
+
+        def differences(h):
+            c0, n = HALVES[h]
+            for t in range(PACK):
+                nc.vector.tensor_tensor(
+                    pa[h][:, t, :], minus_y[t][:].indirect(entries(lists["n1"], c0, n)), y[t][:, c0 : c0 + n], ALU.add
+                )
+                nc.vector.tensor_tensor(
+                    pb[h][:, t, :], y[t][:].indirect(entries(lists["n2"], c0, n)), minus_y[t][:, c0 : c0 + n], ALU.add
+                )
+
+        def piece_of(tiles, c, ts):
+            c0, n = PIECES[c]
+            return tiles[c0 // HALF][:, ts, c0 % HALF : c0 % HALF + n]
+
+        def clamp_below(c, ts):
+            nc.vector.scalar_tensor_tensor(low[c][:, ts, :], piece_of(pb, c, ts), 0.0, piece_of(pa, c, ts), ALU.min, ALU.max)
+
+        def clamp_above(c, ts):
+            nc.vector.scalar_tensor_tensor(z[c][:, ts, :], piece_of(pb, c, ts), 0.0, low[c][:, ts, :], ALU.max, ALU.min)
+
+        def weave(c, woven, planes):
+            src = planes.rearrange("p t s -> p s t")
+            if c == len(PIECES) - 1:
+                nc.vector.tensor_copy(woven[:], src)
+            else:
+                nc.scalar.copy(woven[:], src)
+
+        def quantize(codes, scales, woven):
+            nc.vector.quantize_mx(out=codes.bitcast(FP8X4), scales=scales, in_=woven[:].rearrange("p s t -> p (s t)"))
+
+        h_banks = [[5, 5, 6, 6], [7, 7, 7, 7], [0, 1, 1, 1]]
+
+        def second_product(c):
+            c0, n = PIECES[c]
+            quantize(z_codes[c][:], z_scale[c][:], z_woven[c])
+            accs = {b: bank(b, "h_acc%d_%d" % (c, b)) for b in sorted(set(h_banks[c]))}
+            for t in range(PACK):
+                b = h_banks[c][t]
+                slot = len([u for u in range(t) if h_banks[c][u] == b])
+                acc = accs[b][:, slot * n : (slot + 1) * n]
+                product(acc, 1, t, z_codes[c][:], z_scale[c][:])
+                nc.scalar.activation(minus_h[t][:, c0 : c0 + n], acc, COPY, scale=-1.0)
+                nc.scalar.copy(h_plain[t][:, c0 : c0 + n], acc)
+
+        pairs = [slice(0, 2), slice(2, 4)]
+        every = slice(0, PACK)
+        differences(0)
+        for ts in pairs:
+            clamp_below(0, ts)
+        for ts in pairs:
+            clamp_above(0, ts)
+        weave(0, z_woven[0], z[0][:])
+        differences(1)
+        second_product(0)
+        clamp_below(1, every)
+        clamp_below(2, every)
+        clamp_above(1, every)
+        weave(1, z_woven[1], z[1][:])
+        clamp_above(2, every)
+        second_product(1)
+        weave(2, z_woven[2], z[2][:])
+        second_product(2)
+
+        st = [sb("st%d" % t, [P, S], F32) for t in range(PACK)]
+        hop = [sb("hop%d" % h, [P, PACK, HALF], F32) for h in range(2)]
+        result = [sb("result%d" % c, [P, PACK, n], F32) for c, (c0, n) in enumerate(PIECES)]
+        result_woven = [sb("result_woven%d" % c, [P, n, PACK], BF16) for c, (c0, n) in enumerate(PIECES)]
+        out_codes = sb("out_codes", [P, S], U32)
+        out_scale = sb("out_scale", [P, S], U8)
+        out_rows = out_0.rearrange("(p t) s -> p t s", t=PACK)
+        out_words = words_view(out_1)
+
+        for t in range(PACK):
+            for c0, n in HALVES:
+                nc.vector.tensor_tensor(
+                    st[t][:, c0 : c0 + n],
+                    minus_h[t][:].indirect(entries(lists["n3"], c0, n)),
+                    h_plain[t][:, c0 : c0 + n],
+                    ALU.add,
+                )
+
+        def hops(h):
+            c0, n = HALVES[h]
+            for t in range(PACK):
+                nc.vector.tensor_copy(hop[h][:, t, :], st[t][:].indirect(entries(lists["n4"], c0, n)))
+
+        def larger(c):
+            c0, n = PIECES[c]
+            for t in range(PACK):
+                nc.vector.tensor_tensor(result[c][:, t, :], piece_of(hop, c, t), st[t][:, c0 : c0 + n], ALU.max)
+            nc.sync.dma_start(out_rows[:, :, c0 : c0 + n], result[c][:])
+            weave(c, result_woven[c], result[c][:])
+
+        def planes_out(c):
+            c0, n = PIECES[c]
+            quantize(out_codes[:, c0 : c0 + n], out_scale[:, c0 : c0 + n], result_woven[c])
+            nc.scalar.dma_start(out_words[:, c0 : c0 + n], out_codes[:, c0 : c0 + n].bitcast(I32))
+
+        hops(0)
+        larger(0)
+        hops(1)
+        planes_out(0)
+        larger(1)
+        larger(2)
+        planes_out(1)
+        planes_out(2)
+        for j in range(4):
+            queue = nc.sync if j % 2 == 0 else nc.scalar
+            queue.dma_start(out_2[0, j:16:4, :].bitcast(I32), out_scale[j:P:32, :].bitcast(I32))

@@ -17,8 +17,10 @@ COPY = mybir.ActivationFunctionType.Copy
 
 P = 128
 PACK = 4
+QUADRANT = 32
 HALF = S // 2
 LIST_ROWS = 16
+WHOLE = (0, S)
 HALVES = [(0, HALF), (HALF, HALF)]
 PIECES = [(0, 256), (256, 128), (384, 128)]
 
@@ -32,8 +34,8 @@ def tile_picked_hashminmodhopmx_none_po_kernel(
         keep = ctx.enter_context(tc.tile_pool(name="keep", bufs=1))
         psum = ctx.enter_context(tc.psum_pool(name="psum", bufs=1))
 
-        def sb(name, shape, dtype):
-            return keep.tile(shape, dtype, name=name, align_bytes=64)
+        def sb(name, shape, dtype, tag=""):
+            return keep.tile(shape, dtype, name=name, tag=tag, align_bytes=64)
 
         def bank(number, name):
             return psum.tile([P, 512], F32, name=name, tag="bank%d" % number)
@@ -41,13 +43,17 @@ def tile_picked_hashminmodhopmx_none_po_kernel(
         def words_view(dram):
             return dram[0].rearrange("p n t -> p (n t)").bitcast(I32)
 
-        def entries(lists, start, count):
-            return lists[:, start // LIST_ROWS : (start + count) // LIST_ROWS]
+        def looked_up(window, name, span):
+            start, count = span
+            return window[:].indirect(lists[name][:, start // LIST_ROWS : (start + count) // LIST_ROWS])
+
+        def cols(span):
+            return slice(span[0], span[0] + span[1])
 
         lists = {name: sb("list_" + name, [P, S // LIST_ROWS], U16) for name in ("offs", "n1", "n2", "n3", "n4")}
         x_table = sb("x_table", [P, T], U32)
-        x_scale_table = sb("x_scale_table", [P, T], U8)
-        w_raw = [sb("w_raw%d" % i, [P, 512], U32) for i in range(2)]
+        x_scale_table = sb("x_scale_table", [P, T], U8, tag="early_bytes")
+        w1_raw = sb("w1_raw", [P, H], U32)
         w_scale_raw = sb("w_scale_raw", [P, 512], U8)
         w_codes = [sb("w_codes%d" % i, [P, 512], U32) for i in range(2)]
         w_scale = [sb("w_scale%d" % i, [P, 512], U8) for i in range(2)]
@@ -56,37 +62,34 @@ def tile_picked_hashminmodhopmx_none_po_kernel(
         x_scale = sb("x_scale", [P, S], U8)
         gain = sb("gain", [P, PACK], F32)
         minus_gain = sb("minus_gain", [P, PACK], F32)
-        warm = sb("warm", [P, 8], F32)
-        warm_out = sb("warm_out", [P, 8], F32)
+        plus = [sb("plus%d" % t, [P, S], F32) for t in range(PACK)]
+        minus = [sb("minus%d" % t, [P, S], F32) for t in range(PACK)]
 
-        nc.vector.memset(warm[:], 0.0)
-        nc.vector.memset(x_scale[:].bitcast(I32), 0)
+        def load_weight_scales(dram):
+            for q in range(4):
+                rows = dram[0, 4 * q : 4 * q + 4, :].bitcast(I32)
+                nc.sync.dma_start(
+                    w_scale_raw[QUADRANT * q : QUADRANT * (q + 1), :].bitcast(I32),
+                    rows.unsqueeze(0).broadcast_to([8, 4, 128]),
+                )
 
-        def load_weight_scales(queue, dram, q):
-            rows = dram[0, 4 * q : 4 * q + 4, :].bitcast(I32)
-            queue.dma_start(w_scale_raw[32 * q : 32 * q + 32, :].bitcast(I32), rows.unsqueeze(0).broadcast_to([8, 4, 128]))
-
-        nc.sync.dma_start(
-            x_scale_table[:].bitcast(I32), x_scales[0].bitcast(I32).unsqueeze(1).broadcast_to([16, 8, T // 4])
-        )
-        nc.sync.dma_start(lists["offs"][:], offs)
-        for q in range(4):
-            load_weight_scales(nc.sync if q < 2 else nc.gpsimd, w1_scales, q)
-        nc.sync.dma_start(lists["n1"][:], n1)
-        nc.sync.dma_start(lists["n2"][:], n2)
-        nc.sync.dma_start(w_raw[0][:].bitcast(I32), words_view(w1_words))
-        nc.sync.dma_start(x_table[:].bitcast(I32), words_view(x_words))
-        nc.sync.dma_start(lists["n3"][:], n3)
-        nc.sync.dma_start(lists["n4"][:], n4)
-        nc.sync.dma_start(w_raw[1][:].bitcast(I32), words_view(w2_words))
-        nc.scalar.activation(warm_out[:], warm[:], COPY)
         nc.gpsimd.dma_start(gain[:], gn.rearrange("(p t) o -> p (t o)", t=PACK))
-        nc.gpsimd.tensor_scalar(minus_gain[:], gain[:], -1.0, 0.0, ALU.mult, ALU.add)
+        nc.scalar.activation(minus_gain[:], gain[:], COPY, scale=-1.0)
+        for e in range(2):
+            rows = x_scales[0, e:16:2, :].bitcast(I32)
+            nc.sync.dma_start(x_scale_table[e:P:2, :].bitcast(I32), rows.unsqueeze(1).broadcast_to([8, 8, T // 4]))
+        nc.sync.dma_start(lists["offs"][:], offs)
+        load_weight_scales(w1_scales)
+        nc.sync.dma_start(x_table[:].bitcast(I32), words_view(x_words))
+        nc.sync.dma_start(w1_raw[:].bitcast(I32), words_view(w1_words))
+        for name, dram in (("n1", n1), ("n2", n2), ("n3", n3), ("n4", n4)):
+            nc.sync.dma_start(lists[name][:], dram)
 
-        def deal_words(i):
+
+        def deal_words(i, raw):
             nc.vector.tensor_copy(
                 w_codes[i][:].bitcast(I32).rearrange("p (t m) -> p t m", t=PACK),
-                w_raw[i][:].bitcast(I32).rearrange("p (m t) -> p t m", t=PACK),
+                raw[:].bitcast(I32).rearrange("p (m t) -> p t m", t=PACK),
             )
 
         def deal_scales(i):
@@ -95,46 +98,49 @@ def tile_picked_hashminmodhopmx_none_po_kernel(
                 w_scale_raw[:].rearrange("p (m t) -> p t m", t=PACK),
             )
 
-        nc.vector.tensor_copy(x_scale_picked[:], x_scale_table[:].indirect(lists["offs"][:]))
-        for j in range(4):
-            nc.scalar.dma_start(x_scale[j:P:32, :].bitcast(I32), x_scale_picked[8 * j : P : 32, :].bitcast(I32))
-        deal_words(0)
+        nc.vector.tensor_copy(x_scale_picked[:], looked_up(x_scale_table, "offs", WHOLE))
+        nc.vector.tensor_copy(x_scale[:].bitcast(I32), x_scale_picked[:].bitcast(I32))
+        for e in range(2):
+            nc.sync.dma_start(
+                x_scale[2 + e : P : QUADRANT, :].bitcast(I32), x_scale_picked[16 + e : P : QUADRANT, :].bitcast(I32)
+            )
+        w2_raw = sb("w2_raw", [P, N], U32, tag="early_bytes")
+        nc.sync.dma_start(w2_raw[:].bitcast(I32), words_view(w2_words))
         deal_scales(0)
-        nc.vector.tensor_copy(x_codes[:], x_table[:].indirect(lists["offs"][:]))
-        for q in range(4):
-            load_weight_scales(nc.sync, w2_scales, q)
-        deal_words(1)
+        load_weight_scales(w2_scales)
+        nc.vector.tensor_copy(x_codes[:, cols(HALVES[0])], looked_up(x_table, "offs", HALVES[0]))
+        deal_words(0, w1_raw)
+        nc.vector.tensor_copy(x_codes[:, cols(HALVES[1])], looked_up(x_table, "offs", HALVES[1]))
+        deal_words(1, w2_raw)
         deal_scales(1)
 
         def product(out, i, t, codes, scales):
-            cols = slice(t * P, (t + 1) * P)
+            rows = slice(t * P, (t + 1) * P)
             nc.tensor.matmul_mx(
                 out=out,
-                lhsT=w_codes[i][:, cols].bitcast(FP8X4),
-                lhsT_scale=w_scale[i][:, cols],
+                lhsT=w_codes[i][:, rows].bitcast(FP8X4),
+                lhsT_scale=w_scale[i][:, rows],
                 rhs=codes.bitcast(FP8X4),
                 rhs_scale=scales,
                 start=True,
                 stop=True,
             )
 
-        y = [sb("y%d" % t, [P, S], F32) for t in range(PACK)]
-        minus_y = [sb("minus_y%d" % t, [P, S], F32) for t in range(PACK)]
         first = [bank(h, "y0_%d" % h) for h in range(2)]
-        for h, (c0, n) in enumerate(HALVES):
-            product(first[h][:, 0:n], 0, 0, x_codes[:, c0 : c0 + n], x_scale[:, c0 : c0 + n])
-        nc.scalar.activation(minus_y[0][:, 0:HALF], first[0][:, 0:HALF], COPY, scale=minus_gain[:, 0:1])
-        nc.vector.tensor_scalar(minus_y[0][:, HALF:S], first[1][:, 0:HALF], minus_gain[:, 0:1], None, ALU.mult)
-        nc.scalar.activation(y[0][:, 0:HALF], first[0][:, 0:HALF], COPY, scale=gain[:, 0:1])
-        nc.scalar.activation(y[0][:, HALF:S], first[1][:, 0:HALF], COPY, scale=gain[:, 0:1])
+        for h, span in enumerate(HALVES):
+            product(first[h][:, 0:HALF], 0, 0, x_codes[:, cols(span)], x_scale[:, cols(span)])
+        nc.scalar.activation(minus[0][:, 0:HALF], first[0][:, 0:HALF], COPY, scale=minus_gain[:, 0:1])
+        nc.vector.tensor_scalar(minus[0][:, HALF:S], first[1][:, 0:HALF], minus_gain[:, 0:1], None, ALU.mult)
+        nc.scalar.activation(plus[0][:, 0:HALF], first[0][:, 0:HALF], COPY, scale=gain[:, 0:1])
+        nc.vector.tensor_scalar(plus[0][:, HALF:S], first[1][:, 0:HALF], gain[:, 0:1], None, ALU.mult)
         for t in range(1, PACK):
             acc = bank(1 + t, "y_acc%d" % t)
             product(acc[:], 0, t, x_codes[:], x_scale[:])
-            nc.scalar.activation(minus_y[t][:], acc[:], COPY, scale=minus_gain[:, t : t + 1])
-            nc.scalar.activation(y[t][:], acc[:], COPY, scale=gain[:, t : t + 1])
+            nc.scalar.activation(minus[t][:, 0:S], acc[:], COPY, scale=minus_gain[:, t : t + 1])
+            nc.scalar.activation(plus[t][:, 0:S], acc[:], COPY, scale=gain[:, t : t + 1])
 
-        pa = [sb("pa%d" % h, [P, PACK, HALF], F32) for h in range(2)]
-        pb = [sb("pb%d" % h, [P, PACK, HALF], F32) for h in range(2)]
+        pa = sb("pa", [P, PACK, S], F32)
+        pb = sb("pb", [P, PACK, S], F32)
         low = [sb("low%d" % c, [P, PACK, n], F32) for c, (c0, n) in enumerate(PIECES)]
         z = [sb("z%d" % c, [P, PACK, n], BF16) for c, (c0, n) in enumerate(PIECES)]
         z_woven = [sb("z_woven%d" % c, [P, n, PACK], BF16) for c, (c0, n) in enumerate(PIECES)]
@@ -143,28 +149,20 @@ def tile_picked_hashminmodhopmx_none_po_kernel(
         h_plain = [sb("h%d" % t, [P, S], F32) for t in range(PACK)]
         minus_h = [sb("minus_h%d" % t, [P, S], F32) for t in range(PACK)]
 
-        def differences(h):
-            c0, n = HALVES[h]
-            for t in range(PACK):
-                nc.vector.tensor_tensor(
-                    pa[h][:, t, :], minus_y[t][:].indirect(entries(lists["n1"], c0, n)), y[t][:, c0 : c0 + n], ALU.add
-                )
-                nc.vector.tensor_tensor(
-                    pb[h][:, t, :], y[t][:].indirect(entries(lists["n2"], c0, n)), minus_y[t][:, c0 : c0 + n], ALU.add
-                )
-
-        def piece_of(tiles, c, ts):
-            c0, n = PIECES[c]
-            return tiles[c0 // HALF][:, ts, c0 % HALF : c0 % HALF + n]
+        def differences(t, span):
+            nc.vector.tensor_tensor(pa[:, t, cols(span)], looked_up(minus[t], "n1", span), plus[t][:, cols(span)], ALU.add)
+            nc.vector.tensor_tensor(pb[:, t, cols(span)], looked_up(plus[t], "n2", span), minus[t][:, cols(span)], ALU.add)
 
         def clamp_below(c, ts):
-            nc.vector.scalar_tensor_tensor(low[c][:, ts, :], piece_of(pb, c, ts), 0.0, piece_of(pa, c, ts), ALU.min, ALU.max)
+            at = cols(PIECES[c])
+            nc.vector.scalar_tensor_tensor(low[c][:, ts, :], pb[:, ts, at], 0.0, pa[:, ts, at], ALU.min, ALU.max)
 
         def clamp_above(c, ts):
-            nc.vector.scalar_tensor_tensor(z[c][:, ts, :], piece_of(pb, c, ts), 0.0, low[c][:, ts, :], ALU.max, ALU.min)
+            at = cols(PIECES[c])
+            nc.vector.scalar_tensor_tensor(z[c][:, ts, :], pb[:, ts, at], 0.0, low[c][:, ts, :], ALU.max, ALU.min)
 
         def weave(c, woven, planes):
-            src = planes.rearrange("p t s -> p s t")
+            src = planes[:].rearrange("p t s -> p s t")
             if c == len(PIECES) - 1:
                 nc.vector.tensor_copy(woven[:], src)
             else:
@@ -173,41 +171,49 @@ def tile_picked_hashminmodhopmx_none_po_kernel(
         def quantize(codes, scales, woven):
             nc.vector.quantize_mx(out=codes.bitcast(FP8X4), scales=scales, in_=woven[:].rearrange("p s t -> p (s t)"))
 
-        h_banks = [[5, 5, 6, 6], [7, 7, 7, 7], [0, 1, 1, 1]]
+        def take_h(t, span, acc):
+            nc.scalar.activation(minus_h[t][:, cols(span)], acc, COPY, scale=-1.0)
+            nc.scalar.copy(h_plain[t][:, cols(span)], acc)
+
+        h_first = [bank(5 + c, "h0_%d" % c) for c in range(len(PIECES))]
+        h_rest = {t: bank(1 + t, "h_acc%d" % t) for t in range(1, PACK)}
 
         def second_product(c):
-            c0, n = PIECES[c]
+            span = PIECES[c]
             quantize(z_codes[c][:], z_scale[c][:], z_woven[c])
-            accs = {b: bank(b, "h_acc%d_%d" % (c, b)) for b in sorted(set(h_banks[c]))}
-            for t in range(PACK):
-                b = h_banks[c][t]
-                slot = len([u for u in range(t) if h_banks[c][u] == b])
-                acc = accs[b][:, slot * n : (slot + 1) * n]
-                product(acc, 1, t, z_codes[c][:], z_scale[c][:])
-                nc.scalar.activation(minus_h[t][:, c0 : c0 + n], acc, COPY, scale=-1.0)
-                nc.scalar.copy(h_plain[t][:, c0 : c0 + n], acc)
+            product(h_first[c][:, 0 : span[1]], 1, 0, z_codes[c][:], z_scale[c][:])
+            take_h(0, span, h_first[c][:, 0 : span[1]])
+            for t in range(1, PACK):
+                product(h_rest[t][:, cols(span)], 1, t, z_codes[c][:], z_scale[c][:])
+
+        def take_rest(span):
+            for t in range(1, PACK):
+                take_h(t, span, h_rest[t][:, cols(span)])
 
         pairs = [slice(0, 2), slice(2, 4)]
         every = slice(0, PACK)
-        differences(0)
+        for t in range(PACK):
+            differences(t, HALVES[0])
         for ts in pairs:
             clamp_below(0, ts)
         for ts in pairs:
             clamp_above(0, ts)
-        weave(0, z_woven[0], z[0][:])
-        differences(1)
+        weave(0, z_woven[0], z[0])
+        for t in range(PACK):
+            differences(t, HALVES[1])
         second_product(0)
+        take_rest(HALVES[0])
         clamp_below(1, every)
         clamp_below(2, every)
         clamp_above(1, every)
-        weave(1, z_woven[1], z[1][:])
+        weave(1, z_woven[1], z[1])
         clamp_above(2, every)
+        weave(2, z_woven[2], z[2])
         second_product(1)
-        weave(2, z_woven[2], z[2][:])
         second_product(2)
+        take_rest(HALVES[1])
 
-        st = [sb("st%d" % t, [P, S], F32) for t in range(PACK)]
-        hop = [sb("hop%d" % h, [P, PACK, HALF], F32) for h in range(2)]
+        hop = sb("hop", [P, PACK, S], F32)
         result = [sb("result%d" % c, [P, PACK, n], F32) for c, (c0, n) in enumerate(PIECES)]
         result_woven = [sb("result_woven%d" % c, [P, n, PACK], BF16) for c, (c0, n) in enumerate(PIECES)]
         out_codes = sb("out_codes", [P, S], U32)
@@ -216,34 +222,31 @@ def tile_picked_hashminmodhopmx_none_po_kernel(
         out_words = words_view(out_1)
 
         for t in range(PACK):
-            for c0, n in HALVES:
+            for span in HALVES:
                 nc.vector.tensor_tensor(
-                    st[t][:, c0 : c0 + n],
-                    minus_h[t][:].indirect(entries(lists["n3"], c0, n)),
-                    h_plain[t][:, c0 : c0 + n],
-                    ALU.add,
+                    plus[t][:, cols(span)], looked_up(minus_h[t], "n3", span), h_plain[t][:, cols(span)], ALU.add
                 )
 
-        def hops(h):
-            c0, n = HALVES[h]
-            for t in range(PACK):
-                nc.vector.tensor_copy(hop[h][:, t, :], st[t][:].indirect(entries(lists["n4"], c0, n)))
+        def hops(t, span):
+            nc.vector.tensor_copy(hop[:, t, cols(span)], looked_up(plus[t], "n4", span))
 
         def larger(c):
-            c0, n = PIECES[c]
+            at = cols(PIECES[c])
             for t in range(PACK):
-                nc.vector.tensor_tensor(result[c][:, t, :], piece_of(hop, c, t), st[t][:, c0 : c0 + n], ALU.max)
-            nc.sync.dma_start(out_rows[:, :, c0 : c0 + n], result[c][:])
-            weave(c, result_woven[c], result[c][:])
+                nc.vector.tensor_tensor(result[c][:, t, :], hop[:, t, at], plus[t][:, at], ALU.max)
+            nc.sync.dma_start(out_rows[:, :, at], result[c][:])
+            weave(c, result_woven[c], result[c])
 
         def planes_out(c):
-            c0, n = PIECES[c]
-            quantize(out_codes[:, c0 : c0 + n], out_scale[:, c0 : c0 + n], result_woven[c])
-            nc.scalar.dma_start(out_words[:, c0 : c0 + n], out_codes[:, c0 : c0 + n].bitcast(I32))
+            at = cols(PIECES[c])
+            quantize(out_codes[:, at], out_scale[:, at], result_woven[c])
+            nc.scalar.dma_start(out_words[:, at], out_codes[:, at].bitcast(I32))
 
-        hops(0)
+        for t in range(PACK):
+            hops(t, HALVES[0])
         larger(0)
-        hops(1)
+        for t in range(PACK):
+            hops(t, HALVES[1])
         planes_out(0)
         larger(1)
         larger(2)
@@ -251,4 +254,4 @@ def tile_picked_hashminmodhopmx_none_po_kernel(
         planes_out(2)
         for j in range(4):
             queue = nc.sync if j % 2 == 0 else nc.scalar
-            queue.dma_start(out_2[0, j:16:4, :].bitcast(I32), out_scale[j:P:32, :].bitcast(I32))
+            queue.dma_start(out_2[0, j:16:4, :].bitcast(I32), out_scale[j:P:QUADRANT, :].bitcast(I32))

@@ -20,6 +20,7 @@ PACK = 4
 QUADRANT = 32
 HALF = S // 2
 LIST_ROWS = 16
+WINDOW = 2 * S
 WHOLE = (0, S)
 HALVES = [(0, HALF), (HALF, HALF)]
 PIECES = [(0, 256), (256, 128), (384, 128)]
@@ -62,8 +63,8 @@ def tile_picked_hashminmodhopmx_none_po_kernel(
         x_scale = sb("x_scale", [P, S], U8)
         gain = sb("gain", [P, PACK], F32)
         minus_gain = sb("minus_gain", [P, PACK], F32)
-        plus = [sb("plus%d" % t, [P, S], F32) for t in range(PACK)]
-        minus = [sb("minus%d" % t, [P, S], F32) for t in range(PACK)]
+        plus = [sb("plus%d" % t, [P, WINDOW], F32) for t in range(PACK)]
+        minus = [sb("minus%d" % t, [P, WINDOW], F32) for t in range(PACK)]
 
         def load_weight_scales(dram):
             for q in range(4):
@@ -74,15 +75,20 @@ def tile_picked_hashminmodhopmx_none_po_kernel(
                 )
 
         nc.gpsimd.dma_start(gain[:], gn.rearrange("(p t) o -> p (t o)", t=PACK))
+        for t in range(PACK // 2):
+            for windows in (minus, plus):
+                nc.vector.memset(windows[t][:, S:WINDOW], 0.0)
+                nc.scalar.copy(windows[t + PACK // 2][:, S:WINDOW], windows[t][:, S:WINDOW])
         nc.scalar.activation(minus_gain[:], gain[:], COPY, scale=-1.0)
-        for e in range(2):
-            rows = x_scales[0, e:16:2, :].bitcast(I32)
-            nc.sync.dma_start(x_scale_table[e:P:2, :].bitcast(I32), rows.unsqueeze(1).broadcast_to([8, 8, T // 4]))
+        nc.sync.dma_start(
+            x_scale_table[:].bitcast(I32), x_scales[0].bitcast(I32).unsqueeze(1).broadcast_to([16, 8, T // 4])
+        )
         nc.sync.dma_start(lists["offs"][:], offs)
         load_weight_scales(w1_scales)
+        nc.sync.dma_start(lists["n1"][:], n1)
         nc.sync.dma_start(x_table[:].bitcast(I32), words_view(x_words))
         nc.sync.dma_start(w1_raw[:].bitcast(I32), words_view(w1_words))
-        for name, dram in (("n1", n1), ("n2", n2), ("n3", n3), ("n4", n4)):
+        for name, dram in (("n2", n2), ("n3", n3), ("n4", n4)):
             nc.sync.dma_start(lists[name][:], dram)
 
 
@@ -100,10 +106,8 @@ def tile_picked_hashminmodhopmx_none_po_kernel(
 
         nc.vector.tensor_copy(x_scale_picked[:], looked_up(x_scale_table, "offs", WHOLE))
         nc.vector.tensor_copy(x_scale[:].bitcast(I32), x_scale_picked[:].bitcast(I32))
-        for e in range(2):
-            nc.sync.dma_start(
-                x_scale[2 + e : P : QUADRANT, :].bitcast(I32), x_scale_picked[16 + e : P : QUADRANT, :].bitcast(I32)
-            )
+        for j in range(1, 4):
+            nc.sync.dma_start(x_scale[j:P:QUADRANT, :].bitcast(I32), x_scale_picked[8 * j : P : QUADRANT, :].bitcast(I32))
         w2_raw = sb("w2_raw", [P, N], U32, tag="early_bytes")
         nc.sync.dma_start(w2_raw[:].bitcast(I32), words_view(w2_words))
         deal_scales(0)
@@ -132,7 +136,7 @@ def tile_picked_hashminmodhopmx_none_po_kernel(
         nc.scalar.activation(minus[0][:, 0:HALF], first[0][:, 0:HALF], COPY, scale=minus_gain[:, 0:1])
         nc.vector.tensor_scalar(minus[0][:, HALF:S], first[1][:, 0:HALF], minus_gain[:, 0:1], None, ALU.mult)
         nc.scalar.activation(plus[0][:, 0:HALF], first[0][:, 0:HALF], COPY, scale=gain[:, 0:1])
-        nc.vector.tensor_scalar(plus[0][:, HALF:S], first[1][:, 0:HALF], gain[:, 0:1], None, ALU.mult)
+        nc.scalar.activation(plus[0][:, HALF:S], first[1][:, 0:HALF], COPY, scale=gain[:, 0:1])
         for t in range(1, PACK):
             acc = bank(1 + t, "y_acc%d" % t)
             product(acc[:], 0, t, x_codes[:], x_scale[:])
@@ -147,7 +151,6 @@ def tile_picked_hashminmodhopmx_none_po_kernel(
         z_codes = [sb("z_codes%d" % c, [P, n], U32) for c, (c0, n) in enumerate(PIECES)]
         z_scale = [sb("z_scale%d" % c, [P, n], U8) for c, (c0, n) in enumerate(PIECES)]
         h_plain = [sb("h%d" % t, [P, S], F32) for t in range(PACK)]
-        minus_h = [sb("minus_h%d" % t, [P, S], F32) for t in range(PACK)]
 
         def differences(t, span):
             nc.vector.tensor_tensor(pa[:, t, cols(span)], looked_up(minus[t], "n1", span), plus[t][:, cols(span)], ALU.add)
@@ -172,7 +175,7 @@ def tile_picked_hashminmodhopmx_none_po_kernel(
             nc.vector.quantize_mx(out=codes.bitcast(FP8X4), scales=scales, in_=woven[:].rearrange("p s t -> p (s t)"))
 
         def take_h(t, span, acc):
-            nc.scalar.activation(minus_h[t][:, cols(span)], acc, COPY, scale=-1.0)
+            nc.scalar.activation(minus[t][:, cols(span)], acc, COPY, scale=-1.0)
             nc.scalar.copy(h_plain[t][:, cols(span)], acc)
 
         h_first = [bank(5 + c, "h0_%d" % c) for c in range(len(PIECES))]
@@ -186,33 +189,31 @@ def tile_picked_hashminmodhopmx_none_po_kernel(
             for t in range(1, PACK):
                 product(h_rest[t][:, cols(span)], 1, t, z_codes[c][:], z_scale[c][:])
 
-        def take_rest(span):
-            for t in range(1, PACK):
-                take_h(t, span, h_rest[t][:, cols(span)])
-
         pairs = [slice(0, 2), slice(2, 4)]
         every = slice(0, PACK)
-        for t in range(PACK):
-            differences(t, HALVES[0])
+        differences(0, HALVES[0])
+        for t in range(1, PACK):
+            differences(t, WHOLE)
         for ts in pairs:
             clamp_below(0, ts)
         for ts in pairs:
             clamp_above(0, ts)
         weave(0, z_woven[0], z[0])
-        for t in range(PACK):
-            differences(t, HALVES[1])
+        differences(0, HALVES[1])
+        for ts in reversed(pairs):
+            clamp_below(1, ts)
         second_product(0)
-        take_rest(HALVES[0])
-        clamp_below(1, every)
         clamp_below(2, every)
         clamp_above(1, every)
         weave(1, z_woven[1], z[1])
         clamp_above(2, every)
-        weave(2, z_woven[2], z[2])
         second_product(1)
+        weave(2, z_woven[2], z[2])
         second_product(2)
-        take_rest(HALVES[1])
+        for t in range(1, PACK):
+            take_h(t, WHOLE, h_rest[t][:])
 
+        st = [sb("st%d" % t, [P, S], F32) for t in range(PACK)]
         hop = sb("hop", [P, PACK, S], F32)
         result = [sb("result%d" % c, [P, PACK, n], F32) for c, (c0, n) in enumerate(PIECES)]
         result_woven = [sb("result_woven%d" % c, [P, n, PACK], BF16) for c, (c0, n) in enumerate(PIECES)]
@@ -222,36 +223,30 @@ def tile_picked_hashminmodhopmx_none_po_kernel(
         out_words = words_view(out_1)
 
         for t in range(PACK):
-            for span in HALVES:
-                nc.vector.tensor_tensor(
-                    plus[t][:, cols(span)], looked_up(minus_h[t], "n3", span), h_plain[t][:, cols(span)], ALU.add
-                )
+            nc.vector.tensor_tensor(st[t][:], looked_up(minus[t], "n3", WHOLE), h_plain[t][:], ALU.add)
 
         def hops(t, span):
-            nc.vector.tensor_copy(hop[:, t, cols(span)], looked_up(plus[t], "n4", span))
+            nc.vector.tensor_copy(hop[:, t, cols(span)], looked_up(st[t], "n4", span))
 
         def larger(c):
             at = cols(PIECES[c])
             for t in range(PACK):
-                nc.vector.tensor_tensor(result[c][:, t, :], hop[:, t, at], plus[t][:, at], ALU.max)
+                nc.vector.tensor_tensor(result[c][:, t, :], hop[:, t, at], st[t][:, at], ALU.max)
             nc.sync.dma_start(out_rows[:, :, at], result[c][:])
-            weave(c, result_woven[c], result[c])
 
         def planes_out(c):
             at = cols(PIECES[c])
             quantize(out_codes[:, at], out_scale[:, at], result_woven[c])
             nc.scalar.dma_start(out_words[:, at], out_codes[:, at].bitcast(I32))
 
-        for t in range(PACK):
-            hops(t, HALVES[0])
-        larger(0)
-        for t in range(PACK):
-            hops(t, HALVES[1])
-        planes_out(0)
-        larger(1)
-        larger(2)
-        planes_out(1)
-        planes_out(2)
+        for c, span in enumerate(PIECES):
+            for t in range(PACK):
+                hops(t, span)
+            larger(c)
+            if c > 0:
+                planes_out(c - 1)
+            weave(c, result_woven[c], result[c])
+        planes_out(len(PIECES) - 1)
         for j in range(4):
             queue = nc.sync if j % 2 == 0 else nc.scalar
             queue.dma_start(out_2[0, j:16:4, :].bitcast(I32), out_scale[j:P:QUADRANT, :].bitcast(I32))

@@ -107,7 +107,7 @@ def tile_picked_hashminmodhopmx_none_po_kernel(
         nc.vector.tensor_copy(x_scale_picked[:], looked_up(x_scale_table, "offs", WHOLE))
         nc.vector.tensor_copy(x_scale[:].bitcast(I32), x_scale_picked[:].bitcast(I32))
         for j in range(1, 4):
-            nc.sync.dma_start(x_scale[j:P:QUADRANT, :].bitcast(I32), x_scale_picked[8 * j : P : QUADRANT, :].bitcast(I32))
+            nc.scalar.dma_start(x_scale[j:P:QUADRANT, :].bitcast(I32), x_scale_picked[8 * j : P : QUADRANT, :].bitcast(I32))
         w2_raw = sb("w2_raw", [P, N], U32, tag="early_bytes")
         nc.sync.dma_start(w2_raw[:].bitcast(I32), words_view(w2_words))
         deal_scales(0)
@@ -165,11 +165,12 @@ def tile_picked_hashminmodhopmx_none_po_kernel(
             nc.vector.scalar_tensor_tensor(z[c][:, ts, :], pb[:, ts, at], 0.0, low[c][:, ts, :], ALU.max, ALU.min)
 
         def weave(c, woven, planes):
-            src = planes[:].rearrange("p t s -> p s t")
+            src = planes.rearrange("p t (g i) -> p g t i", i=PACK)
+            dst = woven.rearrange("p (g i) t -> p g t i", i=PACK)
             if c == len(PIECES) - 1:
-                nc.vector.tensor_copy(woven[:], src)
+                nc.vector.tensor_copy(dst, src)
             else:
-                nc.scalar.copy(woven[:], src)
+                nc.scalar.copy(dst, src)
 
         def quantize(codes, scales, woven):
             nc.vector.quantize_mx(out=codes.bitcast(FP8X4), scales=scales, in_=woven[:].rearrange("p s t -> p (s t)"))
@@ -198,55 +199,73 @@ def tile_picked_hashminmodhopmx_none_po_kernel(
             clamp_below(0, ts)
         for ts in pairs:
             clamp_above(0, ts)
-        weave(0, z_woven[0], z[0])
+        weave(0, z_woven[0][:], z[0][:])
         differences(0, HALVES[1])
         for ts in reversed(pairs):
             clamp_below(1, ts)
         second_product(0)
         clamp_below(2, every)
         clamp_above(1, every)
-        weave(1, z_woven[1], z[1])
+        weave(1, z_woven[1][:], z[1][:])
         clamp_above(2, every)
         second_product(1)
-        weave(2, z_woven[2], z[2])
+        weave(2, z_woven[2][:], z[2][:])
         second_product(2)
         for t in range(1, PACK):
             take_h(t, WHOLE, h_rest[t][:])
 
-        st = [sb("st%d" % t, [P, S], F32) for t in range(PACK)]
         hop = sb("hop", [P, PACK, S], F32)
-        result = [sb("result%d" % c, [P, PACK, n], F32) for c, (c0, n) in enumerate(PIECES)]
-        result_woven = [sb("result_woven%d" % c, [P, n, PACK], BF16) for c, (c0, n) in enumerate(PIECES)]
+        result = sb("result", [P, PACK, S], F32)
+        result_woven = [sb("result_woven%d" % h, [P, HALF, PACK], BF16) for h in range(2)]
         out_codes = sb("out_codes", [P, S], U32)
         out_scale = sb("out_scale", [P, S], U8)
         out_rows = out_0.rearrange("(p t) s -> p t s", t=PACK)
         out_words = words_view(out_1)
 
         for t in range(PACK):
-            nc.vector.tensor_tensor(st[t][:], looked_up(minus[t], "n3", WHOLE), h_plain[t][:], ALU.add)
+            for span in HALVES if t == 0 else [WHOLE]:
+                at = cols(span)
+                nc.vector.tensor_tensor(plus[t][:, at], looked_up(minus[t], "n3", span), h_plain[t][:, at], ALU.add)
 
         def hops(t, span):
-            nc.vector.tensor_copy(hop[:, t, cols(span)], looked_up(st[t], "n4", span))
+            nc.vector.tensor_copy(hop[:, t, cols(span)], looked_up(plus[t], "n4", span))
 
-        def larger(c):
-            at = cols(PIECES[c])
-            for t in range(PACK):
-                nc.vector.tensor_tensor(result[c][:, t, :], hop[:, t, at], st[t][:, at], ALU.max)
-            nc.sync.dma_start(out_rows[:, :, at], result[c][:])
+        def larger(t, span):
+            at = cols(span)
+            nc.vector.tensor_tensor(result[:, t, at], hop[:, t, at], plus[t][:, at], ALU.max)
 
-        def planes_out(c):
-            at = cols(PIECES[c])
-            quantize(out_codes[:, at], out_scale[:, at], result_woven[c])
+        def store(ts, span):
+            nc.sync.dma_start(out_rows[:, ts, cols(span)], result[:, ts, cols(span)])
+
+        def weave_result(c):
+            c0, n = PIECES[c]
+            weave(c, result_woven[c0 // HALF][:, c0 % HALF : c0 % HALF + n, :], result[:, :, cols(PIECES[c])])
+
+        def planes_out(h):
+            at = cols(HALVES[h])
+            quantize(out_codes[:, at], out_scale[:, at], result_woven[h])
             nc.scalar.dma_start(out_words[:, at], out_codes[:, at].bitcast(I32))
 
-        for c, span in enumerate(PIECES):
-            for t in range(PACK):
-                hops(t, span)
-            larger(c)
-            if c > 0:
-                planes_out(c - 1)
-            weave(c, result_woven[c], result[c])
-        planes_out(len(PIECES) - 1)
+        hops(0, WHOLE)
+        hops(1, WHOLE)
+        larger(0, WHOLE)
+        hops(2, HALVES[0])
+        larger(1, WHOLE)
+        store(pairs[0], WHOLE)
+        hops(3, HALVES[0])
+        larger(2, HALVES[0])
+        larger(3, HALVES[0])
+        store(pairs[1], HALVES[0])
+        weave_result(0)
+        hops(2, HALVES[1])
+        hops(3, HALVES[1])
+        larger(2, HALVES[1])
+        larger(3, HALVES[1])
+        store(pairs[1], HALVES[1])
+        weave_result(1)
+        planes_out(0)
+        weave_result(2)
+        planes_out(1)
         for j in range(4):
             queue = nc.sync if j % 2 == 0 else nc.scalar
             queue.dma_start(out_2[0, j:16:4, :].bitcast(I32), out_scale[j:P:QUADRANT, :].bitcast(I32))

@@ -18,12 +18,20 @@ COPY = mybir.ActivationFunctionType.Copy
 P = 128
 PACK = 4
 QUADRANT = 32
-HALF = S // 2
+BLOCK_PARTITIONS = 8
+SCALE_ROWS = P // BLOCK_PARTITIONS
 LIST_ROWS = 16
+BANK = 512
 WINDOW = 2 * S
+
+HALF = S // 2
 WHOLE = (0, S)
 HALVES = [(0, HALF), (HALF, HALF)]
-PIECES = [(0, 256), (256, 128), (384, 128)]
+PIECES = [(0, HALF), (HALF, HALF // 2), (HALF + HALF // 2, HALF // 2)]
+PIECE_WIDTHS = [count for first, count in PIECES]
+LAST_PIECE = len(PIECES) - 1
+TILE_PAIRS = [slice(0, 2), slice(2, 4)]
+ALL_TILES = slice(0, PACK)
 
 
 def tile_picked_hashminmodhopmx_none_po_kernel(
@@ -35,53 +43,49 @@ def tile_picked_hashminmodhopmx_none_po_kernel(
         keep = ctx.enter_context(tc.tile_pool(name="keep", bufs=1))
         psum = ctx.enter_context(tc.psum_pool(name="psum", bufs=1))
 
-        def sb(name, shape, dtype, tag=""):
+        def sbuf(name, shape, dtype, tag=""):
             return keep.tile(shape, dtype, name=name, tag=tag, align_bytes=64)
 
         def bank(number, name):
-            return psum.tile([P, 512], F32, name=name, tag="bank%d" % number)
+            return psum.tile([P, BANK], F32, name=name, tag="bank%d" % number)
 
         def words_view(dram):
             return dram[0].rearrange("p n t -> p (n t)").bitcast(I32)
 
         def looked_up(window, name, span):
-            start, count = span
-            return window[:].indirect(lists[name][:, start // LIST_ROWS : (start + count) // LIST_ROWS])
+            first, count = span
+            return window[:].indirect(lists[name][:, first // LIST_ROWS : (first + count) // LIST_ROWS])
 
         def cols(span):
             return slice(span[0], span[0] + span[1])
 
-        lists = {name: sb("list_" + name, [P, S // LIST_ROWS], U16) for name in ("offs", "n1", "n2", "n3", "n4")}
-        x_table = sb("x_table", [P, T], U32)
-        x_scale_table = sb("x_scale_table", [P, T], U8, tag="early_bytes")
-        w1_raw = sb("w1_raw", [P, H], U32)
-        w_scale_raw = sb("w_scale_raw", [P, 512], U8)
-        w_codes = [sb("w_codes%d" % i, [P, 512], U32) for i in range(2)]
-        w_scale = [sb("w_scale%d" % i, [P, 512], U8) for i in range(2)]
-        x_codes = sb("x_codes", [P, S], U32)
-        x_scale_picked = sb("x_scale_picked", [P, S], U8)
-        x_scale = sb("x_scale", [P, S], U8)
-        gain = sb("gain", [P, PACK], F32)
-        minus_gain = sb("minus_gain", [P, PACK], F32)
-        plus = [sb("plus%d" % t, [P, WINDOW], F32) for t in range(PACK)]
-        minus = [sb("minus%d" % t, [P, WINDOW], F32) for t in range(PACK)]
+        lists = {name: sbuf("list_" + name, [P, S // LIST_ROWS], U16) for name in ("offs", "n1", "n2", "n3", "n4")}
+        x_table = sbuf("x_table", [P, T], U32)
+        x_scale_table = sbuf("x_scale_table", [P, T], U8, tag="table_then_w2")
+        w1_raw = sbuf("w1_raw", [P, H], U32)
+        w_scale_raw = sbuf("w_scale_raw", [P, H], U8)
+        w_codes = [sbuf("w_codes%d" % layer, [P, H], U32) for layer in range(2)]
+        w_scale = [sbuf("w_scale%d" % layer, [P, H], U8) for layer in range(2)]
+        x_codes = sbuf("x_codes", [P, S], U32)
+        x_scale_picked = sbuf("x_scale_picked", [P, S], U8)
+        x_scale = sbuf("x_scale", [P, S], U8)
+        gain = sbuf("gain", [P, PACK], F32)
+        minus_gain = sbuf("minus_gain", [P, PACK], F32)
+        plus = [sbuf("plus%d" % t, [P, WINDOW], F32) for t in range(PACK)]
+        minus = [sbuf("minus%d" % t, [P, WINDOW], F32) for t in range(PACK)]
 
         def load_weight_scales(dram):
-            for q in range(4):
+            for q in range(P // QUADRANT):
                 rows = dram[0, 4 * q : 4 * q + 4, :].bitcast(I32)
                 nc.sync.dma_start(
                     w_scale_raw[QUADRANT * q : QUADRANT * (q + 1), :].bitcast(I32),
-                    rows.unsqueeze(0).broadcast_to([8, 4, 128]),
+                    rows.unsqueeze(0).broadcast_to([QUADRANT // 4, 4, H // 4]),
                 )
 
         nc.gpsimd.dma_start(gain[:], gn.rearrange("(p t) o -> p (t o)", t=PACK))
-        for t in range(PACK // 2):
-            for windows in (minus, plus):
-                nc.vector.memset(windows[t][:, S:WINDOW], 0.0)
-                nc.scalar.copy(windows[t + PACK // 2][:, S:WINDOW], windows[t][:, S:WINDOW])
-        nc.scalar.activation(minus_gain[:], gain[:], COPY, scale=-1.0)
         nc.sync.dma_start(
-            x_scale_table[:].bitcast(I32), x_scales[0].bitcast(I32).unsqueeze(1).broadcast_to([16, 8, T // 4])
+            x_scale_table[:].bitcast(I32),
+            x_scales[0].bitcast(I32).unsqueeze(1).broadcast_to([SCALE_ROWS, BLOCK_PARTITIONS, T // 4]),
         )
         nc.sync.dma_start(lists["offs"][:], offs)
         load_weight_scales(w1_scales)
@@ -91,24 +95,32 @@ def tile_picked_hashminmodhopmx_none_po_kernel(
         for name, dram in (("n2", n2), ("n3", n3), ("n4", n4)):
             nc.sync.dma_start(lists[name][:], dram)
 
+        for t in range(PACK // 2):
+            for windows in (minus, plus):
+                nc.vector.memset(windows[t][:, S:WINDOW], 0.0)
+                nc.scalar.copy(windows[t + PACK // 2][:, S:WINDOW], windows[t][:, S:WINDOW])
+        nc.scalar.activation(minus_gain[:], gain[:], COPY, scale=-1.0)
 
-        def deal_words(i, raw):
+        def deal_words(layer, raw):
             nc.vector.tensor_copy(
-                w_codes[i][:].bitcast(I32).rearrange("p (t m) -> p t m", t=PACK),
+                w_codes[layer][:].bitcast(I32).rearrange("p (t m) -> p t m", t=PACK),
                 raw[:].bitcast(I32).rearrange("p (m t) -> p t m", t=PACK),
             )
 
-        def deal_scales(i):
+        def deal_scales(layer):
             nc.vector.tensor_copy(
-                w_scale[i][:].rearrange("p (t m) -> p t m", t=PACK),
+                w_scale[layer][:].rearrange("p (t m) -> p t m", t=PACK),
                 w_scale_raw[:].rearrange("p (m t) -> p t m", t=PACK),
             )
 
         nc.vector.tensor_copy(x_scale_picked[:], looked_up(x_scale_table, "offs", WHOLE))
         nc.vector.tensor_copy(x_scale[:].bitcast(I32), x_scale_picked[:].bitcast(I32))
         for j in range(1, 4):
-            nc.scalar.dma_start(x_scale[j:P:QUADRANT, :].bitcast(I32), x_scale_picked[8 * j : P : QUADRANT, :].bitcast(I32))
-        w2_raw = sb("w2_raw", [P, N], U32, tag="early_bytes")
+            nc.sync.dma_start(
+                x_scale[j:P:QUADRANT, :].bitcast(I32),
+                x_scale_picked[BLOCK_PARTITIONS * j : P : QUADRANT, :].bitcast(I32),
+            )
+        w2_raw = sbuf("w2_raw", [P, N], U32, tag="table_then_w2")
         nc.sync.dma_start(w2_raw[:].bitcast(I32), words_view(w2_words))
         deal_scales(0)
         load_weight_scales(w2_scales)
@@ -118,56 +130,61 @@ def tile_picked_hashminmodhopmx_none_po_kernel(
         deal_words(1, w2_raw)
         deal_scales(1)
 
-        def product(out, i, t, codes, scales):
+        def product(out, layer, t, codes, scales):
             rows = slice(t * P, (t + 1) * P)
             nc.tensor.matmul_mx(
                 out=out,
-                lhsT=w_codes[i][:, rows].bitcast(FP8X4),
-                lhsT_scale=w_scale[i][:, rows],
+                lhsT=w_codes[layer][:, rows].bitcast(FP8X4),
+                lhsT_scale=w_scale[layer][:, rows],
                 rhs=codes.bitcast(FP8X4),
                 rhs_scale=scales,
                 start=True,
                 stop=True,
             )
 
-        first = [bank(h, "y0_%d" % h) for h in range(2)]
-        for h, span in enumerate(HALVES):
-            product(first[h][:, 0:HALF], 0, 0, x_codes[:, cols(span)], x_scale[:, cols(span)])
-        nc.scalar.activation(minus[0][:, 0:HALF], first[0][:, 0:HALF], COPY, scale=minus_gain[:, 0:1])
-        nc.vector.tensor_scalar(minus[0][:, HALF:S], first[1][:, 0:HALF], minus_gain[:, 0:1], None, ALU.mult)
-        nc.scalar.activation(plus[0][:, 0:HALF], first[0][:, 0:HALF], COPY, scale=gain[:, 0:1])
-        nc.scalar.activation(plus[0][:, HALF:S], first[1][:, 0:HALF], COPY, scale=gain[:, 0:1])
+        y_first = [bank(half, "y0_%d" % half) for half in range(2)]
+        for half, span in enumerate(HALVES):
+            product(y_first[half][:, 0:HALF], 0, 0, x_codes[:, cols(span)], x_scale[:, cols(span)])
+        nc.scalar.activation(minus[0][:, 0:HALF], y_first[0][:, 0:HALF], COPY, scale=minus_gain[:, 0:1])
+        nc.vector.tensor_scalar(minus[0][:, HALF:S], y_first[1][:, 0:HALF], minus_gain[:, 0:1], None, ALU.mult)
+        nc.scalar.activation(plus[0][:, 0:HALF], y_first[0][:, 0:HALF], COPY, scale=gain[:, 0:1])
+        nc.scalar.activation(plus[0][:, HALF:S], y_first[1][:, 0:HALF], COPY, scale=gain[:, 0:1])
         for t in range(1, PACK):
-            acc = bank(1 + t, "y_acc%d" % t)
-            product(acc[:], 0, t, x_codes[:], x_scale[:])
-            nc.scalar.activation(minus[t][:, 0:S], acc[:], COPY, scale=minus_gain[:, t : t + 1])
-            nc.scalar.activation(plus[t][:, 0:S], acc[:], COPY, scale=gain[:, t : t + 1])
+            y_rest = bank(1 + t, "y_rest%d" % t)
+            product(y_rest[:], 0, t, x_codes[:], x_scale[:])
+            nc.scalar.activation(minus[t][:, 0:S], y_rest[:], COPY, scale=minus_gain[:, t : t + 1])
+            nc.scalar.activation(plus[t][:, 0:S], y_rest[:], COPY, scale=gain[:, t : t + 1])
 
-        pa = sb("pa", [P, PACK, S], F32)
-        pb = sb("pb", [P, PACK, S], F32)
-        low = [sb("low%d" % c, [P, PACK, n], F32) for c, (c0, n) in enumerate(PIECES)]
-        z = [sb("z%d" % c, [P, PACK, n], BF16) for c, (c0, n) in enumerate(PIECES)]
-        z_woven = [sb("z_woven%d" % c, [P, n, PACK], BF16) for c, (c0, n) in enumerate(PIECES)]
-        z_codes = [sb("z_codes%d" % c, [P, n], U32) for c, (c0, n) in enumerate(PIECES)]
-        z_scale = [sb("z_scale%d" % c, [P, n], U8) for c, (c0, n) in enumerate(PIECES)]
-        h_plain = [sb("h%d" % t, [P, S], F32) for t in range(PACK)]
+        pa = sbuf("pa", [P, PACK, S], F32)
+        pb = sbuf("pb", [P, PACK, S], F32)
+        raised = [sbuf("raised%d" % c, [P, PACK, n], F32) for c, n in enumerate(PIECE_WIDTHS)]
+        z = [sbuf("z%d" % c, [P, PACK, n], BF16) for c, n in enumerate(PIECE_WIDTHS)]
+        z_woven = [sbuf("z_woven%d" % c, [P, n, PACK], BF16) for c, n in enumerate(PIECE_WIDTHS)]
+        z_codes = [sbuf("z_codes%d" % c, [P, n], U32) for c, n in enumerate(PIECE_WIDTHS)]
+        z_scale = [sbuf("z_scale%d" % c, [P, n], U8) for c, n in enumerate(PIECE_WIDTHS)]
+        h_plain = [sbuf("h%d" % t, [P, S], F32) for t in range(PACK)]
 
         def differences(t, span):
-            nc.vector.tensor_tensor(pa[:, t, cols(span)], looked_up(minus[t], "n1", span), plus[t][:, cols(span)], ALU.add)
-            nc.vector.tensor_tensor(pb[:, t, cols(span)], looked_up(plus[t], "n2", span), minus[t][:, cols(span)], ALU.add)
+            at = cols(span)
+            nc.vector.tensor_tensor(pa[:, t, at], looked_up(minus[t], "n1", span), plus[t][:, at], ALU.add)
+            nc.vector.tensor_tensor(pb[:, t, at], looked_up(plus[t], "n2", span), minus[t][:, at], ALU.add)
 
-        def clamp_below(c, ts):
+        def clamp_below(c, tiles):
             at = cols(PIECES[c])
-            nc.vector.scalar_tensor_tensor(low[c][:, ts, :], pb[:, ts, at], 0.0, pa[:, ts, at], ALU.min, ALU.max)
+            nc.vector.scalar_tensor_tensor(
+                raised[c][:, tiles, :], pb[:, tiles, at], 0.0, pa[:, tiles, at], ALU.min, ALU.max
+            )
 
-        def clamp_above(c, ts):
+        def clamp_above(c, tiles):
             at = cols(PIECES[c])
-            nc.vector.scalar_tensor_tensor(z[c][:, ts, :], pb[:, ts, at], 0.0, low[c][:, ts, :], ALU.max, ALU.min)
+            nc.vector.scalar_tensor_tensor(
+                z[c][:, tiles, :], pb[:, tiles, at], 0.0, raised[c][:, tiles, :], ALU.max, ALU.min
+            )
 
         def weave(c, woven, planes):
             src = planes.rearrange("p t (g i) -> p g t i", i=PACK)
             dst = woven.rearrange("p (g i) t -> p g t i", i=PACK)
-            if c == len(PIECES) - 1:
+            if c == LAST_PIECE:
                 nc.vector.tensor_copy(dst, src)
             else:
                 nc.scalar.copy(dst, src)
@@ -180,7 +197,7 @@ def tile_picked_hashminmodhopmx_none_po_kernel(
             nc.scalar.copy(h_plain[t][:, cols(span)], acc)
 
         h_first = [bank(5 + c, "h0_%d" % c) for c in range(len(PIECES))]
-        h_rest = {t: bank(1 + t, "h_acc%d" % t) for t in range(1, PACK)}
+        h_rest = {t: bank(1 + t, "h_rest%d" % t) for t in range(1, PACK)}
 
         def second_product(c):
             span = PIECES[c]
@@ -190,35 +207,33 @@ def tile_picked_hashminmodhopmx_none_po_kernel(
             for t in range(1, PACK):
                 product(h_rest[t][:, cols(span)], 1, t, z_codes[c][:], z_scale[c][:])
 
-        pairs = [slice(0, 2), slice(2, 4)]
-        every = slice(0, PACK)
         differences(0, HALVES[0])
         for t in range(1, PACK):
             differences(t, WHOLE)
-        for ts in pairs:
-            clamp_below(0, ts)
-        for ts in pairs:
-            clamp_above(0, ts)
+        for tiles in TILE_PAIRS:
+            clamp_below(0, tiles)
+        for tiles in TILE_PAIRS:
+            clamp_above(0, tiles)
         weave(0, z_woven[0][:], z[0][:])
         differences(0, HALVES[1])
-        for ts in reversed(pairs):
-            clamp_below(1, ts)
+        for tiles in reversed(TILE_PAIRS):
+            clamp_below(1, tiles)
         second_product(0)
-        clamp_below(2, every)
-        clamp_above(1, every)
+        clamp_below(2, ALL_TILES)
+        clamp_above(1, ALL_TILES)
         weave(1, z_woven[1][:], z[1][:])
-        clamp_above(2, every)
+        clamp_above(2, ALL_TILES)
         second_product(1)
         weave(2, z_woven[2][:], z[2][:])
         second_product(2)
         for t in range(1, PACK):
             take_h(t, WHOLE, h_rest[t][:])
 
-        hop = sb("hop", [P, PACK, S], F32)
-        result = sb("result", [P, PACK, S], F32)
-        result_woven = [sb("result_woven%d" % h, [P, HALF, PACK], BF16) for h in range(2)]
-        out_codes = sb("out_codes", [P, S], U32)
-        out_scale = sb("out_scale", [P, S], U8)
+        hop = sbuf("hop", [P, PACK, S], F32)
+        result = sbuf("result", [P, PACK, S], F32)
+        result_woven = [sbuf("result_woven%d" % half, [P, HALF, PACK], BF16) for half in range(2)]
+        out_codes = sbuf("out_codes", [P, S], U32)
+        out_scale = sbuf("out_scale", [P, S], U8)
         out_rows = out_0.rearrange("(p t) s -> p t s", t=PACK)
         out_words = words_view(out_1)
 
@@ -234,16 +249,17 @@ def tile_picked_hashminmodhopmx_none_po_kernel(
             at = cols(span)
             nc.vector.tensor_tensor(result[:, t, at], hop[:, t, at], plus[t][:, at], ALU.max)
 
-        def store(ts, span):
-            nc.sync.dma_start(out_rows[:, ts, cols(span)], result[:, ts, cols(span)])
+        def store(tiles, span):
+            nc.sync.dma_start(out_rows[:, tiles, cols(span)], result[:, tiles, cols(span)])
 
         def weave_result(c):
-            c0, n = PIECES[c]
-            weave(c, result_woven[c0 // HALF][:, c0 % HALF : c0 % HALF + n, :], result[:, :, cols(PIECES[c])])
+            first, n = PIECES[c]
+            woven = result_woven[first // HALF][:, first % HALF : first % HALF + n, :]
+            weave(c, woven, result[:, :, cols(PIECES[c])])
 
-        def planes_out(h):
-            at = cols(HALVES[h])
-            quantize(out_codes[:, at], out_scale[:, at], result_woven[h])
+        def planes_out(half):
+            at = cols(HALVES[half])
+            quantize(out_codes[:, at], out_scale[:, at], result_woven[half])
             nc.scalar.dma_start(out_words[:, at], out_codes[:, at].bitcast(I32))
 
         hops(0, WHOLE)
@@ -251,21 +267,21 @@ def tile_picked_hashminmodhopmx_none_po_kernel(
         larger(0, WHOLE)
         hops(2, HALVES[0])
         larger(1, WHOLE)
-        store(pairs[0], WHOLE)
+        store(TILE_PAIRS[0], WHOLE)
         hops(3, HALVES[0])
         larger(2, HALVES[0])
         larger(3, HALVES[0])
-        store(pairs[1], HALVES[0])
+        store(TILE_PAIRS[1], HALVES[0])
         weave_result(0)
         hops(2, HALVES[1])
         hops(3, HALVES[1])
         larger(2, HALVES[1])
         larger(3, HALVES[1])
-        store(pairs[1], HALVES[1])
+        store(TILE_PAIRS[1], HALVES[1])
         weave_result(1)
         planes_out(0)
-        weave_result(2)
+        weave_result(LAST_PIECE)
         planes_out(1)
         for j in range(4):
             queue = nc.sync if j % 2 == 0 else nc.scalar
-            queue.dma_start(out_2[0, j:16:4, :].bitcast(I32), out_scale[j:P:QUADRANT, :].bitcast(I32))
+            queue.dma_start(out_2[0, j:SCALE_ROWS:4, :].bitcast(I32), out_scale[j:P:QUADRANT, :].bitcast(I32))

from contextlib import ExitStack

import concourse.mybir as mybir

K, T, S, H, N = 512, 2048, 512, 512, 512
FLOPS = 2 * K * H * S + 2 * H * N * S

F32 = mybir.dt.float32
BF16 = mybir.dt.bfloat16
I32 = mybir.dt.int32
U32 = mybir.dt.uint32
U16 = mybir.dt.uint16
U8 = mybir.dt.uint8
FP8X4 = mybir.dt.float8_e4m3fn_x4
ALU = mybir.AluOpType
COPY = mybir.ActivationFunctionType.Copy

P = 128
PACK = 4
QUADRANT = 32
BLOCK_PARTITIONS = 8
SCALE_ROWS = P // BLOCK_PARTITIONS
LIST_ROWS = 16
BANK = 512
WINDOW = 2 * S

HALF = S // 2
WHOLE = (0, S)
HALVES = [(0, HALF), (HALF, HALF)]
PIECES = [(0, HALF), (HALF, HALF // 2), (HALF + HALF // 2, HALF // 2)]
PIECE_WIDTHS = [count for first, count in PIECES]
LAST_PIECE = len(PIECES) - 1
TILE_PAIRS = [slice(0, 2), slice(2, 4)]
ALL_TILES = slice(0, PACK)


def tile_picked_hashminmodhopmx_none_po_kernel(
    tc, x_words, x_scales, w1_words, w1_scales, gn, w2_words, w2_scales, offs, n1, n2, n3, n4, out_0, out_1, out_2
):
    nc = tc.nc

    with ExitStack() as ctx:
        keep = ctx.enter_context(tc.tile_pool(name="keep", bufs=1))
        psum = ctx.enter_context(tc.psum_pool(name="psum", bufs=1))

        def sbuf(name, shape, dtype, tag=""):
            return keep.tile(shape, dtype, name=name, tag=tag, align_bytes=64)

        def bank(number, name):
            return psum.tile([P, BANK], F32, name=name, tag="bank%d" % number)

        def words_view(dram):
            return dram[0].rearrange("p n t -> p (n t)").bitcast(I32)

        def looked_up(window, name, span):
            first, count = span
            return window[:].indirect(lists[name][:, first // LIST_ROWS : (first + count) // LIST_ROWS])

        def cols(span):
            return slice(span[0], span[0] + span[1])

        lists = {name: sbuf("list_" + name, [P, S // LIST_ROWS], U16) for name in ("offs", "n1", "n2", "n3", "n4")}
        x_table = sbuf("x_table", [P, T], U32)
        x_scale_table = sbuf("x_scale_table", [P, T], U8, tag="table_then_w2")
        w1_raw = sbuf("w1_raw", [P, H], U32)
        w_scale_raw = sbuf("w_scale_raw", [P, H], U8)
        w_codes = [sbuf("w_codes%d" % layer, [P, H], U32) for layer in range(2)]
        w_scale = [sbuf("w_scale%d" % layer, [P, H], U8) for layer in range(2)]
        x_codes = sbuf("x_codes", [P, S], U32)
        x_scale_picked = sbuf("x_scale_picked", [P, S], U8)
        x_scale = sbuf("x_scale", [P, S], U8)
        gain = sbuf("gain", [P, PACK], F32)
        minus_gain = sbuf("minus_gain", [P, PACK], F32)
        plus = [sbuf("plus%d" % t, [P, WINDOW], F32) for t in range(PACK)]
        minus = [sbuf("minus%d" % t, [P, WINDOW], F32) for t in range(PACK)]

        def load_weight_scales(dram):
            for q in range(P // QUADRANT):
                rows = dram[0, 4 * q : 4 * q + 4, :].bitcast(I32)
                nc.sync.dma_start(
                    w_scale_raw[QUADRANT * q : QUADRANT * (q + 1), :].bitcast(I32),
                    rows.unsqueeze(0).broadcast_to([QUADRANT // 4, 4, H // 4]),
                )

        nc.gpsimd.dma_start(gain[:], gn.rearrange("(p t) o -> p (t o)", t=PACK))
        nc.sync.dma_start(
            x_scale_table[:].bitcast(I32),
            x_scales[0].bitcast(I32).unsqueeze(1).broadcast_to([SCALE_ROWS, BLOCK_PARTITIONS, T // 4]),
        )
        nc.sync.dma_start(lists["offs"][:], offs)
        load_weight_scales(w1_scales)
        nc.sync.dma_start(lists["n1"][:], n1)
        nc.sync.dma_start(x_table[:].bitcast(I32), words_view(x_words))
        nc.sync.dma_start(w1_raw[:].bitcast(I32), words_view(w1_words))
        for name, dram in (("n2", n2), ("n3", n3), ("n4", n4)):
            nc.sync.dma_start(lists[name][:], dram)

        for t in range(PACK // 2):
            for windows in (minus, plus):
                nc.vector.memset(windows[t][:, S:WINDOW], 0.0)
                nc.scalar.copy(windows[t + PACK // 2][:, S:WINDOW], windows[t][:, S:WINDOW])
        nc.scalar.activation(minus_gain[:], gain[:], COPY, scale=-1.0)

        def deal_words(layer, raw):
            nc.vector.tensor_copy(
                w_codes[layer][:].bitcast(I32).rearrange("p (t m) -> p t m", t=PACK),
                raw[:].bitcast(I32).rearrange("p (m t) -> p t m", t=PACK),
            )

        def deal_scales(layer):
            nc.vector.tensor_copy(
                w_scale[layer][:].rearrange("p (t m) -> p t m", t=PACK),
                w_scale_raw[:].rearrange("p (m t) -> p t m", t=PACK),
            )

        nc.vector.tensor_copy(x_scale_picked[:], looked_up(x_scale_table, "offs", WHOLE))
        nc.vector.tensor_copy(x_scale[:].bitcast(I32), x_scale_picked[:].bitcast(I32))
        for j in range(1, 4):
            nc.sync.dma_start(
                x_scale[j:P:QUADRANT, :].bitcast(I32),
                x_scale_picked[BLOCK_PARTITIONS * j : P : QUADRANT, :].bitcast(I32),
            )
        w2_raw = sbuf("w2_raw", [P, N], U32, tag="table_then_w2")
        nc.sync.dma_start(w2_raw[:].bitcast(I32), words_view(w2_words))
        deal_scales(0)
        load_weight_scales(w2_scales)
        nc.vector.tensor_copy(x_codes[:, cols(HALVES[0])], looked_up(x_table, "offs", HALVES[0]))
        deal_words(0, w1_raw)
        nc.vector.tensor_copy(x_codes[:, cols(HALVES[1])], looked_up(x_table, "offs", HALVES[1]))
        deal_words(1, w2_raw)
        deal_scales(1)

        def product(out, layer, t, codes, scales):
            rows = slice(t * P, (t + 1) * P)
            nc.tensor.matmul_mx(
                out=out,
                lhsT=w_codes[layer][:, rows].bitcast(FP8X4),
                lhsT_scale=w_scale[layer][:, rows],
                rhs=codes.bitcast(FP8X4),
                rhs_scale=scales,
                start=True,
                stop=True,
            )

        y_first = [bank(half, "y0_%d" % half) for half in range(2)]
        for half, span in enumerate(HALVES):
            product(y_first[half][:, 0:HALF], 0, 0, x_codes[:, cols(span)], x_scale[:, cols(span)])
        nc.scalar.activation(minus[0][:, 0:HALF], y_first[0][:, 0:HALF], COPY, scale=minus_gain[:, 0:1])
        nc.vector.tensor_scalar(minus[0][:, HALF:S], y_first[1][:, 0:HALF], minus_gain[:, 0:1], None, ALU.mult)
        nc.scalar.activation(plus[0][:, 0:HALF], y_first[0][:, 0:HALF], COPY, scale=gain[:, 0:1])
        nc.scalar.activation(plus[0][:, HALF:S], y_first[1][:, 0:HALF], COPY, scale=gain[:, 0:1])
        for t in range(1, PACK):
            y_rest = bank(1 + t, "y_rest%d" % t)
            product(y_rest[:], 0, t, x_codes[:], x_scale[:])
            nc.scalar.activation(minus[t][:, 0:S], y_rest[:], COPY, scale=minus_gain[:, t : t + 1])
            nc.scalar.activation(plus[t][:, 0:S], y_rest[:], COPY, scale=gain[:, t : t + 1])

        pa = sbuf("pa", [P, PACK, S], F32)
        pb = sbuf("pb", [P, PACK, S], F32)
        raised = [sbuf("raised%d" % c, [P, PACK, n], F32) for c, n in enumerate(PIECE_WIDTHS)]
        z = [sbuf("z%d" % c, [P, PACK, n], BF16) for c, n in enumerate(PIECE_WIDTHS)]
        z_woven = [sbuf("z_woven%d" % c, [P, n, PACK], BF16) for c, n in enumerate(PIECE_WIDTHS)]
        z_codes = [sbuf("z_codes%d" % c, [P, n], U32) for c, n in enumerate(PIECE_WIDTHS)]
        z_scale = [sbuf("z_scale%d" % c, [P, n], U8) for c, n in enumerate(PIECE_WIDTHS)]
        h_plain = [sbuf("h%d" % t, [P, S], F32) for t in range(PACK)]

        def differences(t, span):
            at = cols(span)
            nc.vector.tensor_tensor(pa[:, t, at], looked_up(minus[t], "n1", span), plus[t][:, at], ALU.add)
            nc.vector.tensor_tensor(pb[:, t, at], looked_up(plus[t], "n2", span), minus[t][:, at], ALU.add)

        def clamp_below(c, tiles):
            at = cols(PIECES[c])
            nc.vector.scalar_tensor_tensor(
                raised[c][:, tiles, :], pb[:, tiles, at], 0.0, pa[:, tiles, at], ALU.min, ALU.max
            )

        def clamp_above(c, tiles):
            at = cols(PIECES[c])
            nc.vector.scalar_tensor_tensor(
                z[c][:, tiles, :], pb[:, tiles, at], 0.0, raised[c][:, tiles, :], ALU.max, ALU.min
            )

        def weave(c, woven, planes):
            src = planes.rearrange("p t (g i) -> p g t i", i=PACK)
            dst = woven.rearrange("p (g i) t -> p g t i", i=PACK)
            if c == LAST_PIECE:
                nc.vector.tensor_copy(dst, src)
            else:
                nc.scalar.copy(dst, src)

        def quantize(codes, scales, woven):
            nc.vector.quantize_mx(out=codes.bitcast(FP8X4), scales=scales, in_=woven[:].rearrange("p s t -> p (s t)"))

        def take_h(t, span, acc):
            nc.scalar.activation(minus[t][:, cols(span)], acc, COPY, scale=-1.0)
            nc.scalar.copy(h_plain[t][:, cols(span)], acc)

        h_first = [bank(5 + c, "h0_%d" % c) for c in range(len(PIECES))]
        h_rest = {t: bank(1 + t, "h_rest%d" % t) for t in range(1, PACK)}

        def second_product(c):
            span = PIECES[c]
            quantize(z_codes[c][:], z_scale[c][:], z_woven[c])
            product(h_first[c][:, 0 : span[1]], 1, 0, z_codes[c][:], z_scale[c][:])
            take_h(0, span, h_first[c][:, 0 : span[1]])
            for t in range(1, PACK):
                product(h_rest[t][:, cols(span)], 1, t, z_codes[c][:], z_scale[c][:])

        differences(0, HALVES[0])
        for t in range(1, PACK):
            differences(t, WHOLE)
        for tiles in TILE_PAIRS:
            clamp_below(0, tiles)
        for tiles in TILE_PAIRS:
            clamp_above(0, tiles)
        weave(0, z_woven[0][:], z[0][:])
        differences(0, HALVES[1])
        for tiles in reversed(TILE_PAIRS):
            clamp_below(1, tiles)
        second_product(0)
        clamp_below(2, ALL_TILES)
        clamp_above(1, ALL_TILES)
        weave(1, z_woven[1][:], z[1][:])
        clamp_above(2, ALL_TILES)
        second_product(1)
        weave(2, z_woven[2][:], z[2][:])
        second_product(2)
        for t in range(1, PACK):
            take_h(t, WHOLE, h_rest[t][:])

        hop = sbuf("hop", [P, PACK, S], F32)
        result = sbuf("result", [P, PACK, S], F32)
        result_woven = [sbuf("result_woven%d" % half, [P, HALF, PACK], BF16) for half in range(2)]
        out_codes = sbuf("out_codes", [P, S], U32)
        out_scale = sbuf("out_scale", [P, S], U8)
        out_rows = out_0.rearrange("(p t) s -> p t s", t=PACK)
        out_words = words_view(out_1)

        for t in range(PACK):
            for span in HALVES if t == 0 else [WHOLE]:
                at = cols(span)
                nc.vector.tensor_tensor(plus[t][:, at], looked_up(minus[t], "n3", span), h_plain[t][:, at], ALU.add)

        def hops(t, span):
            nc.vector.tensor_copy(hop[:, t, cols(span)], looked_up(plus[t], "n4", span))

        def larger(t, span):
            at = cols(span)
            nc.vector.tensor_tensor(result[:, t, at], hop[:, t, at], plus[t][:, at], ALU.max)

        def store(tiles, span):
            nc.sync.dma_start(out_rows[:, tiles, cols(span)], result[:, tiles, cols(span)])

        def weave_result(c):
            first, n = PIECES[c]
            woven = result_woven[first // HALF][:, first % HALF : first % HALF + n, :]
            weave(c, woven, result[:, :, cols(PIECES[c])])

        def planes_out(half):
            at = cols(HALVES[half])
            quantize(out_codes[:, at], out_scale[:, at], result_woven[half])
            nc.scalar.dma_start(out_words[:, at], out_codes[:, at].bitcast(I32))

        hops(0, WHOLE)
        hops(1, WHOLE)
        larger(0, WHOLE)
        hops(2, HALVES[0])
        larger(1, WHOLE)
        store(TILE_PAIRS[0], WHOLE)
        hops(3, HALVES[0])
        larger(2, HALVES[0])
        larger(3, HALVES[0])
        store(TILE_PAIRS[1], HALVES[0])
        weave_result(0)
        hops(2, HALVES[1])
        hops(3, HALVES[1])
        larger(2, HALVES[1])
        larger(3, HALVES[1])
        store(TILE_PAIRS[1], HALVES[1])
        weave_result(1)
        planes_out(0)
        weave_result(LAST_PIECE)
        planes_out(1)
        for j in range(4):
            queue = nc.sync if j % 2 == 0 else nc.scalar
            queue.dma_start(out_2[0, j:SCALE_ROWS:4, :].bitcast(I32), out_scale[j:P:QUADRANT, :].bitcast(I32))
